import numpy as np
import ml_dtypes


def mxq(x, axis, fmt="e4m3"):
    dtype, down = {"e4m3": (ml_dtypes.float8_e4m3fn, 7), "e5m2": (ml_dtypes.float8_e5m2, 14)}[fmt]
    v = np.moveaxis(np.asarray(x, np.float32).astype(ml_dtypes.bfloat16).astype(np.float64), axis, -1)
    blocks = v.reshape(v.shape[:-1] + (-1, 32))
    amax = np.abs(blocks).max(-1, keepdims=True)
    byte = np.maximum(np.where(amax > 0, np.frexp(amax)[1] - 1 + 127, 0) - down, 1)
    scale = np.exp2(byte - 127.0)
    codes = (blocks / scale).astype(np.float32).astype(dtype).astype(np.float64)
    return np.moveaxis((codes * scale).reshape(v.shape), -1, axis)


WIDE = False


def mx_kscale(k):
    if not WIDE:
        return np.ones(k)
    levels = np.array([10, -10, 5, -5, 0])
    if k % 512:
        return np.exp2(np.random.permutation(np.resize(levels, k // 32))).repeat(32)
    a = np.empty((k // 512, 16))
    for p in range(k // 512):
        a[p, :8] = np.random.permutation(np.resize(levels, 8))
        for g in range(8):
            far = levels[np.abs(levels - a[p, g]) >= 10]
            a[p, g + 8] = far[np.random.randint(len(far))]
    return np.exp2(a.ravel()).repeat(32)


def f64(x):
    return np.asarray(x).astype(np.float64)


def striped(idx):
    return np.tile(idx.reshape(-1, 16).T, (8, 1)).astype(np.uint16)


def unstriped(offs):
    return offs[:16].T.reshape(-1).astype(np.int64)


E2M1 = np.array([0.0, 0.5, 1.0, 1.5, 2.0, 3.0, 4.0, 6.0, -0.0, -0.5, -1.0, -1.5, -2.0, -3.0, -4.0, -6.0])


def pack_weight(w, fmt):
    k, n = w.shape
    w = f64(np.asarray(w, np.float32).astype(ml_dtypes.bfloat16)).reshape(k // 32, 32, n)
    amax = np.abs(w).max(1)
    if fmt == "e4m3":
        byte = np.frexp(amax)[1] - 1 + 127 - 7
    else:
        mant, ex = np.frexp(amax / 6.0)
        byte = np.where(mant > 0.5, ex, ex - 1) + 127
    byte = np.clip(np.where(amax > 0, byte, 1), 1, 254)
    scaled = (w * np.exp2(127.0 - byte)[:, None, :]).reshape(k, n).astype(np.float32)
    by_word = np.ascontiguousarray(scaled.reshape(k // 512, 128, 4, n).transpose(0, 1, 3, 2))
    if fmt == "e4m3":
        words = by_word.astype(ml_dtypes.float8_e4m3fn).view(np.uint8)
    else:
        c = by_word.astype(ml_dtypes.float4_e2m1fn).view(np.uint8) & 0xF
        words = (c[..., 0::2] | (c[..., 1::2] << 4)).reshape(k // 512, 128, 2 * n)
    return np.ascontiguousarray(words), np.ascontiguousarray(byte.astype(np.uint8).reshape(k // 512, 16, n))


def unpack_weight(words, scales, fmt):
    g, _, n = scales.shape
    words = np.ascontiguousarray(words).reshape(g, 128, n, -1)
    if fmt == "e4m3":
        vals = words.view(ml_dtypes.float8_e4m3fn).astype(np.float64)
    else:
        nib = np.empty((g, 128, n, 4), np.uint8)
        nib[..., 0::2] = words & 0xF
        nib[..., 1::2] = words >> 4
        vals = E2M1[nib]
    vals = vals * np.repeat(np.exp2(scales.astype(np.float64) - 127.0), 8, axis=1)[..., None]
    return vals.transpose(0, 1, 3, 2).reshape(g * 512, n)


def gelu(v):
    return 0.5 * v * (1.0 + np.tanh(np.sqrt(2.0 / np.pi) * (v + 0.044715 * v**3)))


def bf(x):
    return np.asarray(x, np.float32).astype(ml_dtypes.bfloat16)


def planes(Y):
    n, m = Y.shape
    b = f64(bf(Y)).reshape(n // 32, 32, m)
    amax = np.abs(b).max(1)
    byte = np.clip(np.where(amax > 0, np.frexp(amax)[1] - 1 + 127 - 7, 1), 1, 254)
    codes = (b * np.exp2(127.0 - byte)[:, None, :]).reshape(n, m).astype(np.float32).astype(ml_dtypes.float8_e4m3fn).view(np.uint8)
    words = codes.reshape(n // 512, 128, 4, m).transpose(0, 1, 3, 2)
    return np.ascontiguousarray(words), np.ascontiguousarray(byte.astype(np.uint8).reshape(n // 512, 16, m))


K, T, S, H, T2, P, N = 512, 4096, 1024, 1024, 2048, 1024, 384


def setup_inputs():
    n = np.random.standard_normal
    s = mx_kscale(K)[:, None]
    u = mx_kscale(H)[:, None]
    d = {}
    d["tab_words"], d["tab_scales"] = pack_weight(n((K, T)) * s, "e4m3")
    d["offs"] = striped(np.random.permutation(T)[:S])
    d["w1"] = (n((K, H)) / s * u.T / K**0.5).astype(np.float32)
    d["w2_words"], d["w2_scales"] = pack_weight(n((K, H)) / s / K**0.5, "e2m1")
    d["survey_map"] = (0.8 * n((H, S)) * u).astype(np.float32)
    d["wgs"] = np.exp(0.3 * n((128, S))).astype(np.float32)
    d["page0"] = (n((H, T2)) * u).astype(np.float32)
    d["offs2"] = striped(np.random.permutation(T2)[:S])
    d["offs3"] = striped(np.random.permutation(T2)[:P])
    d["cap"] = (0.5 * np.exp(0.6 * n(H)) * u[:, 0]).astype(np.float32)
    d["w3"] = (1.5 * n((H, N)) / u / H**0.5).astype(np.float32)
    d["w4_words"], d["w4_scales"] = pack_weight(1.5 * n((H, N)) / u / H**0.5, "e4m3")
    return d


def reference(tab_words, tab_scales, offs, w1, w2_words, w2_scales, survey_map, wgs, page0, offs2, offs3, cap, w3, w4_words, w4_scales):
    v = unpack_weight(tab_words, tab_scales, "e4m3")[:, unstriped(offs)]
    mapped = (mxq(f64(w1), 0, "e4m3").T @ v) + f64(survey_map)
    h = mapped * (unpack_weight(w2_words, w2_scales, "e2m1").T @ v)
    page = f64(page0).copy()
    page[:, unstriped(offs2)] = np.tile(f64(wgs), (H // 128, 1)) * h
    x = np.minimum(page[:, unstriped(offs3)], f64(cap)[:, None])
    xq = mxq(x, 0, "e4m3")
    top = mxq(f64(w3), 0, "e4m3").T @ xq
    spread = unpack_weight(w4_words, w4_scales, "e4m3").T @ xq
    y = top / (1.0 + np.abs(spread))
    words, scales = planes(page)
    return y, page, words, scales

@@ -1,0 +1,370 @@
+from contextlib import ExitStack
+
+import concourse.mybir as mybir
+
+K, T, S, H, T2, M, N = 512, 4096, 1024, 1024, 2048, 1024, 384
+FLOPS = 2 * 2 * K * H * S + 2 * 2 * H * N * M
+
+F32 = mybir.dt.float32
+BF16 = mybir.dt.bfloat16
+I32 = mybir.dt.int32
+U32 = mybir.dt.uint32
+U16 = mybir.dt.uint16
+U8 = mybir.dt.uint8
+FP8X4 = mybir.dt.float8_e4m3fn_x4
+FP4X4 = mybir.dt.float4_e2m1fn_x4
+ALU = mybir.AluOpType
+ACT = mybir.ActivationFunctionType
+
+P = 128
+PACK = 4
+GROUPS = H // (P * PACK)
+SLICES = GROUPS * PACK
+BANK = 512
+QUADS = 4
+
+
+def tile_list_parcel_page_scores_kernel(
+    tc, tab_words, tab_scales, offs, w1, w2_words, w2_scales, survey_map, wgs, page0, offs2, offs3, cap, w3,
+    w4_words, w4_scales, out_0, out_1, out_2, out_3,
+):
+    nc = tc.nc
+    with ExitStack() as ctx:
+        lists = ctx.enter_context(tc.tile_pool(name="lists", bufs=1))
+        sb = ctx.enter_context(tc.tile_pool(name="sb", bufs=1))
+        psum = ctx.enter_context(tc.psum_pool(name="psum", bufs=8))
+
+        def tile(name, shape, dtype, tag=None, bufs=1):
+            return sb.tile(shape, dtype, name=name, tag=tag or name, bufs=bufs, align_bytes=64)
+
+        def half(h):
+            return slice(h * BANK, (h + 1) * BANK)
+
+        def list_half(h):
+            return slice(h * BANK // 16, (h + 1) * BANK // 16)
+
+        table = tile("table", [P, T], U32, tag="table_pairs")
+        nc.sync.dma_start(table[:].bitcast(I32), tab_words[0].rearrange("p t i -> p (t i)").bitcast(I32))
+        w2_raw = tile("w2_raw", [P, 2 * H], U8)
+        nc.scalar.dma_start(w2_raw[:].bitcast(I32), w2_words[0].bitcast(I32))
+        w2_scale_raw = tile("w2_scale_raw", [P, H], U8)
+        for q in range(QUADS):
+            nc.scalar.dma_start(
+                w2_scale_raw[32 * q : 32 * q + 32, :].bitcast(I32),
+                w2_scales[0, 4 * q : 4 * q + 4, :].bitcast(I32).partition_broadcast(8),
+            )
+        pick = lists.tile([P, S // 16], U16, name="pick")
+        nc.sync.dma_start(pick[:], offs)
+        table_scale = tile("table_scale", [P, T], U8, tag="scales")
+        nc.vector.memset(table_scale[:].bitcast(I32), 0)
+        for q in range(QUADS):
+            nc.gpsimd.dma_start(
+                table_scale[32 * q : 32 * q + 4, :].bitcast(I32), tab_scales[0, 4 * q : 4 * q + 4, :].bitcast(I32)
+            )
+
+        w1_rows = w1.rearrange("(p i) c -> p i c", i=PACK)
+        w1_raw = [tile("w1_raw%d" % g, [P, PACK, BANK], F32, tag="woven%d" % g) for g in range(GROUPS)]
+        survey_rows = survey_map.rearrange("(g p t) j -> g t p j", p=P, t=PACK)
+        page_rows = page0.rearrange("(g p t) m -> g t p m", p=P, t=PACK)
+        out_rows = out_1.rearrange("(g p t) m -> g t p m", p=P, t=PACK)
+        wgs_rows = wgs.rearrange("(q t) j -> q t j", t=PACK)
+        factor = [tile("factor0", [P, 1, S], F32), tile("factor1", [P, 1, S], F32), tile("factor23", [P, 2, S], F32)]
+        factor_first = [0, 1, 2]
+        survey = []
+        page = []
+
+        def load_survey(s):
+            survey.append(tile("survey%d" % s, [P, S], F32, tag="survey_y", bufs=4))
+            nc.sync.dma_start(survey[s][:], survey_rows[s // PACK, s % PACK])
+
+        def load_page(s):
+            page.append(tile("page%d" % s, [P, T2], F32))
+            nc.sync.dma_start(page[s][:], page_rows[s // PACK, s % PACK])
+
+        def load_factor(i):
+            first, count = factor_first[i], factor[i].shape[1]
+            for q in range(QUADS):
+                nc.sync.dma_start(factor[i][32 * q : 32 * q + 32, :, :], wgs_rows[:, first : first + count, :])
+
+        def factor_of(t):
+            return factor[min(t, 2)][:, max(t - 2, 0), :]
+
+        nc.sync.dma_start(w1_raw[0][:], w1_rows[:, :, half(0)])
+        load_survey(0)
+        load_factor(0)
+        put = lists.tile([P, S // 16], U16, name="put")
+        nc.sync.dma_start(put[:], offs2)
+        load_page(0)
+        load_survey(1)
+        load_factor(1)
+        fetch = lists.tile([P, M // 16], U16, name="fetch")
+        nc.sync.dma_start(fetch[:], offs3)
+        caps = tile("caps", [P, GROUPS, PACK], F32)
+        nc.sync.dma_start(caps[:], cap.rearrange("(g p t) -> p g t", p=P, t=PACK))
+        load_page(1)
+        load_survey(2)
+        load_factor(2)
+        load_page(2)
+        nc.sync.dma_start(w1_raw[1][:], w1_rows[:, :, half(1)])
+        load_survey(3)
+        load_page(3)
+        w3_raw = tile("w3_raw", [P, GROUPS, PACK, N], F32, tag="w3raw_capped1")
+        nc.sync.dma_start(w3_raw[:], w3.rearrange("(g p i) n -> p g i n", p=P, i=PACK))
+        w4_codes = tile("w4_codes", [P, GROUPS * N], U32)
+        nc.sync.dma_start(
+            w4_codes[:].bitcast(I32).rearrange("p (g n) -> p g n", g=GROUPS),
+            w4_words.rearrange("g p n i -> p g (n i)").bitcast(I32),
+        )
+        w4_scale = tile("w4_scale", [P, GROUPS * N], U8)
+        nc.vector.memset(w4_scale[:].bitcast(I32), 0)
+        for q in range(QUADS):
+            nc.sync.dma_start(
+                w4_scale[32 * q : 32 * q + 4, :].bitcast(I32).rearrange("p (g n) -> p g n", g=GROUPS),
+                w4_scales[:, 4 * q : 4 * q + 4, :].rearrange("g r n -> r g n").bitcast(I32),
+            )
+        for s in range(PACK, SLICES):
+            load_survey(s)
+            load_page(s)
+
+        warm = tile("warm", [P, 1], F32)
+        nc.vector.memset(warm[:], 1.0)
+        nc.scalar.activation(warm[:], warm[:], ACT.Abs_reciprocal_sqrt)
+
+        w2_codes = tile("w2_codes", [P, 2 * H], U8)
+        nc.vector.tensor_copy(
+            w2_codes[:].rearrange("p (g t q b) -> p g t q b", g=GROUPS, t=PACK, b=2),
+            w2_raw[:].rearrange("p (g q t b) -> p g t q b", g=GROUPS, t=PACK, b=2),
+        )
+        w2_scale = tile("w2_scale", [P, H], U8)
+        nc.vector.tensor_copy(
+            w2_scale[:].rearrange("p (g t q) -> p g t q", g=GROUPS, t=PACK),
+            w2_scale_raw[:].rearrange("p (g q t) -> p g t q", g=GROUPS, t=PACK),
+        )
+        v_codes = [tile("v_codes%d" % h, [P, BANK], U32) for h in range(2)]
+        v_scale = [tile("v_scale%d" % h, [P, BANK], U8) for h in range(2)]
+        for h in range(2):
+            nc.vector.tensor_copy(v_codes[h][:], table[:].indirect(pick[:, list_half(h)]))
+            nc.vector.tensor_copy(v_scale[h][:], table_scale[:].indirect(pick[:, list_half(h)]))
+
+        w_cols = H + GROUPS * N
+        w_bf = tile("w_bf", [P, PACK * w_cols], BF16, tag="wide_bf")
+        w_codes = tile("w_codes", [P, w_cols], U32)
+        w_scale = tile("w_scale", [P, w_cols], U8)
+
+        def round_w1(g, t0, t1):
+            dst = w_bf[:, g * PACK * BANK : (g + 1) * PACK * BANK].rearrange("p (t q i) -> p q t i", t=PACK, i=PACK)
+            src = w1_raw[g][:].rearrange("p i (q t) -> p q t i", t=PACK)
+            nc.scalar.copy(dst[:, :, t0:t1, :], src[:, :, t0:t1, :])
+
+        def round_w3():
+            nc.scalar.copy(
+                w_bf[:, PACK * H :].rearrange("p (g c j i) -> p g c i j", g=GROUPS, j=PACK, i=PACK),
+                w3_raw[:].rearrange("p g i (c j) -> p g c i j", j=PACK),
+            )
+
+        def quantize_w(c0, c1):
+            nc.vector.quantize_mx(
+                out=w_codes[:, c0:c1].bitcast(FP8X4), scales=w_scale[:, c0:c1], in_=w_bf[:, c0 * PACK : c1 * PACK]
+            )
+
+        round_w1(0, 0, 1)
+        quantize_w(0, P)
+        round_w1(0, 1, PACK)
+        quantize_w(P, 2 * P)
+        quantize_w(2 * P, 4 * P)
+
+        values = {}
+        capped = [tile("capped0", [P, PACK * M], BF16), None]
+        pairs = {}
+        x_codes = {}
+        x_bf = {}
+        x_scale = [tile("x_scale%d" % g, [P, M], U8) for g in range(GROUPS)]
+        plane_scale = tile("plane_scale", [P, GROUPS * T2], U8, tag="scales")
+        values_slot = ["work0", "work1", "work0", "work1", "work0", "work1", "wide_bf", "woven0"]
+        fetched_slot = ["work0", "work1", "work0", "work1", "x_codes0", "plane_codes0", "plane_codes1", "w3raw_capped1"]
+
+        def products(s, h):
+            cols = slice(s * P, (s + 1) * P)
+            first = psum.tile([P, BANK], F32, name="first", tag="bank")
+            nc.tensor.matmul_mx(
+                out=first[:], lhsT=w_codes[:, cols].bitcast(FP8X4), lhsT_scale=w_scale[:, cols],
+                rhs=v_codes[h][:].bitcast(FP8X4), rhs_scale=v_scale[h][:], start=True, stop=True,
+            )
+            second = psum.tile([P, BANK], F32, name="second", tag="bank")
+            nc.tensor.matmul_mx(
+                out=second[:], lhsT=w2_codes[:, 2 * s * P : 2 * (s + 1) * P].bitcast(FP4X4),
+                lhsT_scale=w2_scale[:, cols],
+                rhs=v_codes[h][:].bitcast(FP8X4), rhs_scale=v_scale[h][:], start=True, stop=True,
+            )
+            return first, second
+
+        def make_values(s):
+            values[s] = tile("values%d" % s, [P, S], F32, tag=values_slot[s])
+            first_sb = tile("first_sb%d" % s, [P, S], F32, tag="first_sb", bufs=2)
+            second_sb = tile("second_sb%d" % s, [P, S], F32, tag="second_sb", bufs=3)
+            val, wg = values[s], factor_of(s % PACK)
+            on_vector = 1 if s == 0 else 0
+            for h in range(2):
+                first, second = products(s, h)
+                c = half(h)
+                if h < on_vector:
+                    nc.vector.tensor_tensor(val[:, c], first[:], survey[s][:, c], ALU.add)
+                    nc.vector.tensor_tensor(second_sb[:, c], second[:], wg[:, c], ALU.mult)
+                    nc.vector.tensor_tensor(val[:, c], val[:, c], second_sb[:, c], ALU.mult)
+                else:
+                    nc.scalar.copy(first_sb[:, c], first[:])
+                    nc.scalar.copy(second_sb[:, c], second[:])
+            c = slice(on_vector * BANK, S)
+            nc.gpsimd.tensor_tensor(val[:, c], first_sb[:, c], survey[s][:, c], ALU.add)
+            nc.gpsimd.tensor_tensor(second_sb[:, c], second_sb[:, c], wg[:, c], ALU.mult)
+            nc.gpsimd.tensor_tensor(val[:, c], val[:, c], second_sb[:, c], ALU.mult)
+
+        def scatter(s):
+            if s == 0:
+                for h in range(2):
+                    nc.vector.tensor_copy(page[s][:].indirect(put[:, list_half(h)]), values[s][:, half(h)])
+            else:
+                nc.vector.tensor_copy(page[s][:].indirect(put[:]), values[s][:])
+
+        def quantize_x(g, cols):
+            nc.vector.quantize_mx(
+                out=x_codes[g][:, cols].bitcast(FP8X4), scales=x_scale[g][:, cols],
+                in_=x_bf[g][:, cols.start * PACK : cols.stop * PACK],
+            )
+
+        def weave_x(g, count):
+            x_bf[g] = tile("x_bf%d" % g, [P, PACK * M], BF16, tag="wide_bf")
+            src = capped[g][:].rearrange("p (t c i) -> p c t i", t=count, i=PACK)
+            dst = x_bf[g][:].rearrange("p (c i t) -> p c t i", t=PACK, i=PACK)
+            nc.scalar.copy(dst[:, :, 0:count, :], src)
+
+        def fetch_and_cap(s):
+            g, t = divmod(s, PACK)
+            fetched = tile("fetched%d" % s, [P, M], F32, tag=fetched_slot[s])
+            if s == PACK:
+                capped[1] = tile("capped1", [P, (PACK - 1) * M], BF16, tag="w3raw_capped1")
+            if s == SLICES - 1:
+                x_codes[g] = tile("x_codes1", [P, M], U32)
+                last = x_bf[g][:].rearrange("p (m t) -> p m t", t=PACK)
+                for h in range(2):
+                    nc.vector.tensor_copy(fetched[:, half(h)], page[s][:].indirect(fetch[:, list_half(h)]))
+                    nc.vector.tensor_scalar(last[:, half(h), t], fetched[:, half(h)], caps[:, g, t : t + 1], None, ALU.min)
+                    quantize_x(g, half(h))
+            else:
+                nc.vector.tensor_copy(fetched[:], page[s][:].indirect(fetch[:]))
+                nc.vector.tensor_scalar(capped[g][:, t * M : (t + 1) * M], fetched[:], caps[:, g, t : t + 1], None, ALU.min)
+
+        def round_page(s):
+            g, t = divmod(s, PACK)
+            if t == 0:
+                pairs[g] = tile("pairs%d" % g, [P, PACK * T2], BF16, tag="table_pairs")
+            dst = pairs[g][:].rearrange("p (u m e) -> p u m e", u=2, e=2)
+            nc.scalar.copy(dst[:, t // 2, :, t % 2], page[s][:])
+            nc.sync.dma_start(out_rows[g, t], page[s][:])
+
+        woven = {}
+        width = T2 // 2
+
+        def weave_page(g, h, copy):
+            woven[g, h] = tile("woven%d_%d" % (g, h), [P, PACK * width], BF16, tag="woven%d" % h)
+            copy(
+                woven[g, h][:].bitcast(F32).rearrange("p (m u) -> p m u", u=2),
+                pairs[g][:].bitcast(F32).rearrange("p (u m) -> p m u", u=2)[:, h * width : (h + 1) * width, :],
+            )
+
+        def page_planes(g, h):
+            codes = tile("plane_codes%d_%d" % (g, h), [P, width], U32, tag="plane_codes%d" % h)
+            nc.vector.quantize_mx(
+                out=codes[:].bitcast(FP8X4),
+                scales=plane_scale[:, g * T2 + h * width : g * T2 + (h + 1) * width],
+                in_=woven[g, h][:],
+            )
+            nc.sync.dma_start(
+                out_2[g, :, h * width : (h + 1) * width, :].rearrange("p m t -> p (m t)").bitcast(I32),
+                codes[:].bitcast(I32),
+            )
+
+        units = [(h, b) for h in range(2) for b in range(N // P)]
+        top, spread = {}, {}
+
+        def score_pass(sums, codes, scale, first, unit, g):
+            h, b = unit
+            if g == 0:
+                sums[unit] = psum.tile([P, BANK], F32, name="score", tag="bank")
+            cols = slice(first + g * N + b * P, first + g * N + (b + 1) * P)
+            nc.tensor.matmul_mx(
+                out=sums[unit][:], lhsT=codes[:, cols].bitcast(FP8X4), lhsT_scale=scale[:, cols],
+                rhs=x_codes[g][:, half(h)].bitcast(FP8X4), rhs_scale=x_scale[g][:, half(h)],
+                start=(g == 0), stop=(g == GROUPS - 1),
+            )
+
+        def top_pass(unit, g):
+            score_pass(top, w_codes, w_scale, H, unit, g)
+
+        def spread_pass(unit, g):
+            score_pass(spread, w4_codes, w4_scale, 0, unit, g)
+
+        def finish(unit, square_on_scalar):
+            h, b = unit
+            size = tile("size", [P, BANK], F32, tag="first_sb", bufs=2)
+            nc.scalar.activation(size[:], spread[unit][:], ACT.Abs)
+            root = tile("root", [P, BANK], F32, tag="second_sb", bufs=3)
+            nc.scalar.activation(root[:], size[:], ACT.Abs_reciprocal_sqrt, bias=1.0)
+            y = tile("y", [P, BANK], F32, tag="survey_y", bufs=4)
+            if square_on_scalar:
+                nc.scalar.activation(root[:], root[:], ACT.Square)
+                nc.vector.tensor_tensor(y[:], top[unit][:], root[:], ALU.mult)
+            else:
+                nc.vector.tensor_tensor(y[:], top[unit][:], root[:], ALU.mult)
+                nc.vector.tensor_tensor(y[:], y[:], root[:], ALU.mult)
+            nc.sync.dma_start(out_0[b * P : (b + 1) * P, half(h)], y[:])
+
+        make_values(0)
+        make_values(1)
+        for s in range(SLICES):
+            scatter(s)
+            if s == SLICES - 1:
+                round_page(s)
+            fetch_and_cap(s)
+            if s == 4:
+                x_codes[0] = tile("x_codes0", [P, M], U32)
+                quantize_x(0, slice(0, M))
+            if s in (5, 6):
+                page_planes(0, s - 5)
+            if s + 2 < SLICES:
+                make_values(s + 2)
+            if s < SLICES - 1:
+                round_page(s)
+            if s == 0:
+                round_w1(1, 0, PACK)
+                quantize_w(4 * P, 6 * P)
+            if s == 1:
+                round_w3()
+                quantize_w(6 * P, w_cols)
+            if s == PACK - 1:
+                weave_x(0, PACK)
+                weave_page(0, 0, nc.scalar.copy)
+                weave_page(0, 1, nc.scalar.copy)
+            if s == SLICES - 2:
+                weave_x(1, PACK - 1)
+                for unit in units:
+                    spread_pass(unit, 0)
+                for unit in units[:2]:
+                    top_pass(unit, 0)
+
+        for h in range(2):
+            for unit in units[3 * h : 3 * h + 3]:
+                spread_pass(unit, 1)
+            for i in range(3 * h, 3 * h + 3):
+                if i >= 2:
+                    top_pass(units[i], 0)
+                top_pass(units[i], 1)
+                finish(units[i], i < 4)
+        for h in range(2):
+            weave_page(1, h, nc.vector.tensor_copy)
+            page_planes(1, h)
+        for q in range(QUADS):
+            nc.sync.dma_start(
+                out_3[:, 4 * q : 4 * q + 4, :].rearrange("g r m -> r g m").bitcast(I32),
+                plane_scale[32 * q : 32 * q + 4, :].bitcast(I32).rearrange("p (g m) -> p g m", g=GROUPS),
+            )

@@ -94,22 +94,23 @@ def tile_list_parcel_page_scores_kernel(
         load_factor(0)
         put = lists.tile([P, S // 16], U16, name="put")
         nc.sync.dma_start(put[:], offs2)
-        load_page(0)
         load_survey(1)
+        load_page(0)
         load_factor(1)
         fetch = lists.tile([P, M // 16], U16, name="fetch")
         nc.sync.dma_start(fetch[:], offs3)
         caps = tile("caps", [P, GROUPS, PACK], F32)
         nc.sync.dma_start(caps[:], cap.rearrange("(g p t) -> p g t", p=P, t=PACK))
-        load_page(1)
         load_survey(2)
         load_factor(2)
-        load_page(2)
         nc.sync.dma_start(w1_raw[1][:], w1_rows[:, :, half(1)])
+        load_page(1)
         load_survey(3)
-        load_page(3)
         w3_raw = tile("w3_raw", [P, GROUPS, PACK, N], F32, tag="w3raw_capped1")
         nc.sync.dma_start(w3_raw[:], w3.rearrange("(g p i) n -> p g i n", p=P, i=PACK))
+        load_page(2)
+        load_survey(4)
+        load_page(3)
         w4_codes = tile("w4_codes", [P, GROUPS * N], U32)
         nc.sync.dma_start(
             w4_codes[:].bitcast(I32).rearrange("p (g n) -> p g n", g=GROUPS),
@@ -123,7 +124,8 @@ def tile_list_parcel_page_scores_kernel(
                 w4_scales[:, 4 * q : 4 * q + 4, :].rearrange("g r n -> r g n").bitcast(I32),
             )
         for s in range(PACK, SLICES):
-            load_survey(s)
+            if s + 1 < SLICES:
+                load_survey(s + 1)
             load_page(s)
 
         warm = tile("warm", [P, 1], F32)
@@ -146,30 +148,51 @@ def tile_list_parcel_page_scores_kernel(
             nc.vector.tensor_copy(v_codes[h][:], table[:].indirect(pick[:, list_half(h)]))
             nc.vector.tensor_copy(v_scale[h][:], table_scale[:].indirect(pick[:, list_half(h)]))
 
-        w_cols = H + GROUPS * N
-        w_bf = tile("w_bf", [P, PACK * w_cols], BF16, tag="wide_bf")
-        w_codes = tile("w_codes", [P, w_cols], U32)
-        w_scale = tile("w_scale", [P, w_cols], U8)
+        w_scale = tile("w_scale", [P, H + GROUPS * N], U8)
+        w_first = [0, 4 * P, H, H + GROUPS * N]
+        w_bf_slot = ["wide_bf", "work2", "work1"]
+        w_bf, w_codes = {}, {}
 
-        def round_w1(g, t0, t1):
-            dst = w_bf[:, g * PACK * BANK : (g + 1) * PACK * BANK].rearrange("p (t q i) -> p q t i", t=PACK, i=PACK)
+        def w_part(col):
+            return max(i for i in range(3) if w_first[i] <= col)
+
+        def w_operand(col):
+            part = w_part(col)
+            first = col - w_first[part]
+            return w_codes[part][:, first : first + P].bitcast(FP8X4), w_scale[:, col : col + P]
+
+        def open_w(part):
+            cols = w_first[part + 1] - w_first[part]
+            w_bf[part] = tile("w_bf%d" % part, [P, PACK * cols], BF16, tag=w_bf_slot[part])
+
+        def round_w1(s0, s1):
+            part = w_part(s0 * P)
+            first = s0 * P - w_first[part]
+            g, t0 = divmod(s0, PACK)
+            dst = w_bf[part][:, first * PACK : (first + (s1 - s0) * P) * PACK]
             src = w1_raw[g][:].rearrange("p i (q t) -> p q t i", t=PACK)
-            nc.scalar.copy(dst[:, :, t0:t1, :], src[:, :, t0:t1, :])
+            nc.scalar.copy(dst.rearrange("p (t q i) -> p q t i", q=P, i=PACK), src[:, :, t0 : t0 + s1 - s0, :])
 
         def round_w3():
             nc.scalar.copy(
-                w_bf[:, PACK * H :].rearrange("p (g c j i) -> p g c i j", g=GROUPS, j=PACK, i=PACK),
+                w_bf[2][:].rearrange("p (g c j i) -> p g c i j", g=GROUPS, j=PACK, i=PACK),
                 w3_raw[:].rearrange("p g i (c j) -> p g c i j", j=PACK),
             )
 
         def quantize_w(c0, c1):
+            part = w_part(c0)
+            if part not in w_codes:
+                w_codes[part] = tile("w_codes%d" % part, [P, w_first[part + 1] - w_first[part]], U32)
+            lo, hi = c0 - w_first[part], c1 - w_first[part]
             nc.vector.quantize_mx(
-                out=w_codes[:, c0:c1].bitcast(FP8X4), scales=w_scale[:, c0:c1], in_=w_bf[:, c0 * PACK : c1 * PACK]
+                out=w_codes[part][:, lo:hi].bitcast(FP8X4), scales=w_scale[:, c0:c1],
+                in_=w_bf[part][:, lo * PACK : hi * PACK],
             )
 
-        round_w1(0, 0, 1)
+        open_w(0)
+        round_w1(0, 1)
         quantize_w(0, P)
-        round_w1(0, 1, PACK)
+        round_w1(1, PACK)
         quantize_w(P, 2 * P)
         quantize_w(2 * P, 4 * P)
 
@@ -180,14 +203,15 @@ def tile_list_parcel_page_scores_kernel(
         x_bf = {}
         x_scale = [tile("x_scale%d" % g, [P, M], U8) for g in range(GROUPS)]
         plane_scale = tile("plane_scale", [P, GROUPS * T2], U8, tag="scales")
-        values_slot = ["work0", "work1", "work0", "work1", "work0", "work1", "wide_bf", "woven0"]
-        fetched_slot = ["work0", "work1", "work0", "work1", "x_codes0", "plane_codes0", "plane_codes1", "w3raw_capped1"]
+        values_slot = ["work0", "work1", "work0", "work2", "work0", "work2", "work1", "wide_bf"]
+        fetched_slot = ["work0", "w_codes1", "work0", "work2", "w_codes2", "x_codes0", "plane_codes", "w3raw_capped1"]
 
         def products(s, h):
             cols = slice(s * P, (s + 1) * P)
             first = psum.tile([P, BANK], F32, name="first", tag="bank")
+            codes, scale = w_operand(s * P)
             nc.tensor.matmul_mx(
-                out=first[:], lhsT=w_codes[:, cols].bitcast(FP8X4), lhsT_scale=w_scale[:, cols],
+                out=first[:], lhsT=codes, lhsT_scale=scale,
                 rhs=v_codes[h][:].bitcast(FP8X4), rhs_scale=v_scale[h][:], start=True, stop=True,
             )
             second = psum.tile([P, BANK], F32, name="second", tag="bank")
@@ -200,24 +224,24 @@ def tile_list_parcel_page_scores_kernel(
 
         def make_values(s):
             values[s] = tile("values%d" % s, [P, S], F32, tag=values_slot[s])
-            first_sb = tile("first_sb%d" % s, [P, S], F32, tag="first_sb", bufs=2)
-            second_sb = tile("second_sb%d" % s, [P, S], F32, tag="second_sb", bufs=3)
+            mapped = tile("mapped%d" % s, [P, S], F32, tag="mapped", bufs=2)
+            second_sb = tile("second_sb%d" % s, [P, S], F32, tag="second_sb", bufs=2)
             val, wg = values[s], factor_of(s % PACK)
-            on_vector = 1 if s == 0 else 0
-            for h in range(2):
-                first, second = products(s, h)
-                c = half(h)
-                if h < on_vector:
-                    nc.vector.tensor_tensor(val[:, c], first[:], survey[s][:, c], ALU.add)
-                    nc.vector.tensor_tensor(second_sb[:, c], second[:], wg[:, c], ALU.mult)
-                    nc.vector.tensor_tensor(val[:, c], val[:, c], second_sb[:, c], ALU.mult)
-                else:
-                    nc.scalar.copy(first_sb[:, c], first[:])
-                    nc.scalar.copy(second_sb[:, c], second[:])
-            c = slice(on_vector * BANK, S)
-            nc.gpsimd.tensor_tensor(val[:, c], first_sb[:, c], survey[s][:, c], ALU.add)
-            nc.gpsimd.tensor_tensor(second_sb[:, c], second_sb[:, c], wg[:, c], ALU.mult)
-            nc.gpsimd.tensor_tensor(val[:, c], val[:, c], second_sb[:, c], ALU.mult)
+            c0, c1 = half(0), half(1)
+            first, second = products(s, 0)
+            nc.vector.tensor_tensor(mapped[:, c0], first[:], survey[s][:, c0], ALU.add)
+            if s == 0:
+                nc.vector.tensor_tensor(val[:, c0], second[:], wg[:, c0], ALU.mult)
+                nc.vector.tensor_tensor(val[:, c0], val[:, c0], mapped[:, c0], ALU.mult)
+            else:
+                nc.scalar.copy(second_sb[:, c0], second[:])
+            first, second = products(s, 1)
+            nc.scalar.copy(second_sb[:, c1], second[:])
+            nc.scalar.copy(mapped[:, c1], first[:])
+            c = c1 if s == 0 else slice(0, S)
+            nc.gpsimd.tensor_tensor(val[:, c], second_sb[:, c], wg[:, c], ALU.mult)
+            nc.gpsimd.tensor_tensor(mapped[:, c1], mapped[:, c1], survey[s][:, c1], ALU.add)
+            nc.gpsimd.tensor_tensor(val[:, c], val[:, c], mapped[:, c], ALU.mult)
 
         def scatter(s):
             if s == 0:
@@ -226,31 +250,30 @@ def tile_list_parcel_page_scores_kernel(
             else:
                 nc.vector.tensor_copy(page[s][:].indirect(put[:]), values[s][:])
 
-        def quantize_x(g, cols):
-            nc.vector.quantize_mx(
-                out=x_codes[g][:, cols].bitcast(FP8X4), scales=x_scale[g][:, cols],
-                in_=x_bf[g][:, cols.start * PACK : cols.stop * PACK],
-            )
+        def quantize_x(g, cols, woven_x):
+            nc.vector.quantize_mx(out=x_codes[g][:, cols].bitcast(FP8X4), scales=x_scale[g][:, cols], in_=woven_x[:])
 
-        def weave_x(g, count):
-            x_bf[g] = tile("x_bf%d" % g, [P, PACK * M], BF16, tag="wide_bf")
+        def weave_x(name, slot, g, count, cols):
+            woven_x = tile(name, [P, PACK * (cols.stop - cols.start)], BF16, tag=slot)
             src = capped[g][:].rearrange("p (t c i) -> p c t i", t=count, i=PACK)
-            dst = x_bf[g][:].rearrange("p (c i t) -> p c t i", t=PACK, i=PACK)
-            nc.scalar.copy(dst[:, :, 0:count, :], src)
+            dst = woven_x[:].rearrange("p (c i t) -> p c t i", t=PACK, i=PACK)
+            nc.scalar.copy(dst[:, :, 0:count, :], src[:, cols.start // PACK : cols.stop // PACK, :, :])
+            return woven_x
 
         def fetch_and_cap(s):
             g, t = divmod(s, PACK)
-            fetched = tile("fetched%d" % s, [P, M], F32, tag=fetched_slot[s])
             if s == PACK:
                 capped[1] = tile("capped1", [P, (PACK - 1) * M], BF16, tag="w3raw_capped1")
             if s == SLICES - 1:
                 x_codes[g] = tile("x_codes1", [P, M], U32)
-                last = x_bf[g][:].rearrange("p (m t) -> p m t", t=PACK)
                 for h in range(2):
-                    nc.vector.tensor_copy(fetched[:, half(h)], page[s][:].indirect(fetch[:, list_half(h)]))
-                    nc.vector.tensor_scalar(last[:, half(h), t], fetched[:, half(h)], caps[:, g, t : t + 1], None, ALU.min)
-                    quantize_x(g, half(h))
+                    fetched = tile("fetched7_%d" % h, [P, BANK], F32, tag=("w3raw_capped1", "work1")[h])
+                    last = x_bf[g][h][:].rearrange("p (m t) -> p m t", t=PACK)
+                    nc.vector.tensor_copy(fetched[:], page[s][:].indirect(fetch[:, list_half(h)]))
+                    nc.vector.tensor_scalar(last[:, :, t], fetched[:], caps[:, g, t : t + 1], None, ALU.min)
+                    quantize_x(g, half(h), x_bf[g][h])
             else:
+                fetched = tile("fetched%d" % s, [P, M], F32, tag=fetched_slot[s])
                 nc.vector.tensor_copy(fetched[:], page[s][:].indirect(fetch[:]))
                 nc.vector.tensor_scalar(capped[g][:, t * M : (t + 1) * M], fetched[:], caps[:, g, t : t + 1], None, ALU.min)
 
@@ -262,7 +285,7 @@ def tile_list_parcel_page_scores_kernel(
             nc.scalar.copy(dst[:, t // 2, :, t % 2], page[s][:])
             nc.sync.dma_start(out_rows[g, t], page[s][:])
 
-        woven = {}
+        woven, plane_codes = {}, {}
         width = T2 // 2
 
         def weave_page(g, h, copy):
@@ -273,85 +296,103 @@ def tile_list_parcel_page_scores_kernel(
             )
 
         def page_planes(g, h):
-            codes = tile("plane_codes%d_%d" % (g, h), [P, width], U32, tag="plane_codes%d" % h)
+            if h == 0:
+                plane_codes[g] = tile("plane_codes%d" % g, [P, T2], U32, tag=("plane_codes", "page0")[g])
+            codes = plane_codes[g][:, h * width : (h + 1) * width]
             nc.vector.quantize_mx(
-                out=codes[:].bitcast(FP8X4),
+                out=codes.bitcast(FP8X4),
                 scales=plane_scale[:, g * T2 + h * width : g * T2 + (h + 1) * width],
                 in_=woven[g, h][:],
             )
             nc.sync.dma_start(
                 out_2[g, :, h * width : (h + 1) * width, :].rearrange("p m t -> p (m t)").bitcast(I32),
-                codes[:].bitcast(I32),
+                codes.bitcast(I32),
             )
 
         units = [(h, b) for h in range(2) for b in range(N // P)]
         top, spread = {}, {}
 
-        def score_pass(sums, codes, scale, first, unit, g):
-            h, b = unit
+        def score_pass(sums, codes, scale, unit, g):
+            h = unit[0]
             if g == 0:
                 sums[unit] = psum.tile([P, BANK], F32, name="score", tag="bank")
-            cols = slice(first + g * N + b * P, first + g * N + (b + 1) * P)
             nc.tensor.matmul_mx(
-                out=sums[unit][:], lhsT=codes[:, cols].bitcast(FP8X4), lhsT_scale=scale[:, cols],
+                out=sums[unit][:], lhsT=codes, lhsT_scale=scale,
                 rhs=x_codes[g][:, half(h)].bitcast(FP8X4), rhs_scale=x_scale[g][:, half(h)],
                 start=(g == 0), stop=(g == GROUPS - 1),
             )
 
         def top_pass(unit, g):
-            score_pass(top, w_codes, w_scale, H, unit, g)
+            score_pass(top, *w_operand(H + g * N + unit[1] * P), unit, g)
 
         def spread_pass(unit, g):
-            score_pass(spread, w4_codes, w4_scale, 0, unit, g)
+            cols = slice(g * N + unit[1] * P, g * N + (unit[1] + 1) * P)
+            score_pass(spread, w4_codes[:, cols].bitcast(FP8X4), w4_scale[:, cols], unit, g)
 
         def finish(unit, square_on_scalar):
             h, b = unit
-            size = tile("size", [P, BANK], F32, tag="first_sb", bufs=2)
-            nc.scalar.activation(size[:], spread[unit][:], ACT.Abs)
-            root = tile("root", [P, BANK], F32, tag="second_sb", bufs=3)
-            nc.scalar.activation(root[:], size[:], ACT.Abs_reciprocal_sqrt, bias=1.0)
-            y = tile("y", [P, BANK], F32, tag="survey_y", bufs=4)
+            if b == 0:
+                scores[h] = tile("scores%d" % h, [P, N // P * BANK], F32, tag="page%d" % (1 + h))
+            work = scores[h][:, b * BANK : (b + 1) * BANK]
+            nc.scalar.activation(work, spread[unit][:], ACT.Abs)
+            nc.scalar.activation(work, work, ACT.Abs_reciprocal_sqrt, bias=1.0)
             if square_on_scalar:
-                nc.scalar.activation(root[:], root[:], ACT.Square)
-                nc.vector.tensor_tensor(y[:], top[unit][:], root[:], ALU.mult)
+                nc.scalar.activation(work, work, ACT.Square)
+                nc.vector.tensor_tensor(work, top[unit][:], work, ALU.mult)
             else:
-                nc.vector.tensor_tensor(y[:], top[unit][:], root[:], ALU.mult)
-                nc.vector.tensor_tensor(y[:], y[:], root[:], ALU.mult)
-            nc.sync.dma_start(out_0[b * P : (b + 1) * P, half(h)], y[:])
+                once = tile("once", [P, BANK], F32, tag="mapped", bufs=2)
+                nc.vector.tensor_tensor(once[:], top[unit][:], work, ALU.mult)
+                nc.vector.tensor_tensor(work, once[:], work, ALU.mult)
+            nc.sync.dma_start(out_0[b * P : (b + 1) * P, half(h)], work)
 
+        scores = {}
         make_values(0)
         make_values(1)
+        open_w(1)
+        round_w1(PACK, SLICES)
         for s in range(SLICES):
             scatter(s)
             if s == SLICES - 1:
                 round_page(s)
             fetch_and_cap(s)
+            if s == 1:
+                quantize_w(w_first[1], w_first[2])
+            if s == 3:
+                x_bf[0] = weave_x("x_bf0", "wide_bf", 0, PACK, slice(0, M))
             if s == 4:
+                quantize_w(H, H + BANK)
+                quantize_w(H + BANK, w_first[3])
+            if s == 5:
                 x_codes[0] = tile("x_codes0", [P, M], U32)
-                quantize_x(0, slice(0, M))
-            if s in (5, 6):
-                page_planes(0, s - 5)
+                quantize_x(0, slice(0, M), x_bf[0])
+            if s == 6:
+                page_planes(0, 0)
+                page_planes(0, 1)
+                x_bf[1] = [weave_x("x_bf1_%d" % h, ("work1", "work0")[h], 1, PACK - 1, half(h)) for h in range(2)]
             if s + 2 < SLICES:
                 make_values(s + 2)
             if s < SLICES - 1:
                 round_page(s)
-            if s == 0:
-                round_w1(1, 0, PACK)
-                quantize_w(4 * P, 6 * P)
             if s == 1:
+                open_w(2)
                 round_w3()
-                quantize_w(6 * P, w_cols)
-            if s == PACK - 1:
-                weave_x(0, PACK)
+            if s == 3:
                 weave_page(0, 0, nc.scalar.copy)
                 weave_page(0, 1, nc.scalar.copy)
-            if s == SLICES - 2:
-                weave_x(1, PACK - 1)
+            if s == 6:
                 for unit in units:
                     spread_pass(unit, 0)
                 for unit in units[:2]:
                     top_pass(unit, 0)
 
+        for part in range(2):
+            weave_page(1, part, nc.vector.tensor_copy)
+            page_planes(1, part)
+        for q in range(QUADS):
+            nc.sync.dma_start(
+                out_3[:, 4 * q : 4 * q + 4, :].rearrange("g r m -> r g m").bitcast(I32),
+                plane_scale[32 * q : 32 * q + 4, :].bitcast(I32).rearrange("p (g m) -> p g m", g=GROUPS),
+            )
         for h in range(2):
             for unit in units[3 * h : 3 * h + 3]:
                 spread_pass(unit, 1)
@@ -359,12 +400,4 @@ def tile_list_parcel_page_scores_kernel(
                 if i >= 2:
                     top_pass(units[i], 0)
                 top_pass(units[i], 1)
-                finish(units[i], i < 4)
-        for h in range(2):
-            weave_page(1, h, nc.vector.tensor_copy)
-            page_planes(1, h)
-        for q in range(QUADS):
-            nc.sync.dma_start(
-                out_3[:, 4 * q : 4 * q + 4, :].rearrange("g r m -> r g m").bitcast(I32),
-                plane_scale[32 * q : 32 * q + 4, :].bitcast(I32).rearrange("p (g m) -> p g m", g=GROUPS),
-            )
+                finish(units[i], i < 6)

@@ -20,8 +20,13 @@ P = 128
 PACK = 4
 GROUPS = H // (P * PACK)
 SLICES = GROUPS * PACK
+LAST = SLICES - 1
 BANK = 512
+BANKS = 8
 QUADS = 4
+LIST_ROWS = 16
+PLANE_PART = T2 // 2
+AHEAD = 2
 
 
 def tile_list_parcel_page_scores_kernel(
@@ -32,59 +37,63 @@ def tile_list_parcel_page_scores_kernel(
     with ExitStack() as ctx:
         lists = ctx.enter_context(tc.tile_pool(name="lists", bufs=1))
         sb = ctx.enter_context(tc.tile_pool(name="sb", bufs=1))
-        psum = ctx.enter_context(tc.psum_pool(name="psum", bufs=8))
+        psum = ctx.enter_context(tc.psum_pool(name="psum", bufs=BANKS))
 
-        def tile(name, shape, dtype, tag=None, bufs=1):
-            return sb.tile(shape, dtype, name=name, tag=tag or name, bufs=bufs, align_bytes=64)
+        def tile(name, shape, dtype, slot=None, bufs=1):
+            return sb.tile(shape, dtype, name=name, tag=slot or name, bufs=bufs, align_bytes=64)
 
         def half(h):
             return slice(h * BANK, (h + 1) * BANK)
 
         def list_half(h):
-            return slice(h * BANK // 16, (h + 1) * BANK // 16)
+            return slice(h * BANK // LIST_ROWS, (h + 1) * BANK // LIST_ROWS)
 
-        table = tile("table", [P, T], U32, tag="table_pairs")
+        def quadrant(q, rows):
+            return slice(32 * q, 32 * q + rows)
+
+        def scale_rows(q):
+            return slice(4 * q, 4 * q + 4)
+
+        table = tile("table", [P, T], U32, slot="table_then_pairs")
         nc.sync.dma_start(table[:].bitcast(I32), tab_words[0].rearrange("p t i -> p (t i)").bitcast(I32))
         w2_raw = tile("w2_raw", [P, 2 * H], U8)
         nc.scalar.dma_start(w2_raw[:].bitcast(I32), w2_words[0].bitcast(I32))
         w2_scale_raw = tile("w2_scale_raw", [P, H], U8)
         for q in range(QUADS):
             nc.scalar.dma_start(
-                w2_scale_raw[32 * q : 32 * q + 32, :].bitcast(I32),
-                w2_scales[0, 4 * q : 4 * q + 4, :].bitcast(I32).partition_broadcast(8),
+                w2_scale_raw[quadrant(q, 32), :].bitcast(I32),
+                w2_scales[0, scale_rows(q), :].bitcast(I32).partition_broadcast(8),
             )
-        pick = lists.tile([P, S // 16], U16, name="pick")
+        pick = lists.tile([P, S // LIST_ROWS], U16, name="pick")
         nc.sync.dma_start(pick[:], offs)
-        table_scale = tile("table_scale", [P, T], U8, tag="scales")
+        table_scale = tile("table_scale", [P, T], U8, slot="scales")
         nc.vector.memset(table_scale[:].bitcast(I32), 0)
         for q in range(QUADS):
             nc.gpsimd.dma_start(
-                table_scale[32 * q : 32 * q + 4, :].bitcast(I32), tab_scales[0, 4 * q : 4 * q + 4, :].bitcast(I32)
+                table_scale[quadrant(q, 4), :].bitcast(I32), tab_scales[0, scale_rows(q), :].bitcast(I32)
             )
 
-        w1_rows = w1.rearrange("(p i) c -> p i c", i=PACK)
-        w1_raw = [tile("w1_raw%d" % g, [P, PACK, BANK], F32, tag="woven%d" % g) for g in range(GROUPS)]
+        w1_rows = w1.rearrange("(p i) r -> p i r", i=PACK)
+        w1_raw = [tile("w1_raw%d" % g, [P, PACK, BANK], F32, slot="woven%d" % g) for g in range(GROUPS)]
         survey_rows = survey_map.rearrange("(g p t) j -> g t p j", p=P, t=PACK)
         page_rows = page0.rearrange("(g p t) m -> g t p m", p=P, t=PACK)
         out_rows = out_1.rearrange("(g p t) m -> g t p m", p=P, t=PACK)
         wgs_rows = wgs.rearrange("(q t) j -> q t j", t=PACK)
         factor = [tile("factor0", [P, 1, S], F32), tile("factor1", [P, 1, S], F32), tile("factor23", [P, 2, S], F32)]
-        factor_first = [0, 1, 2]
-        survey = []
-        page = []
+        survey, page = [], []
 
         def load_survey(s):
-            survey.append(tile("survey%d" % s, [P, S], F32, tag="survey_y", bufs=4))
+            survey.append(tile("survey%d" % s, [P, S], F32, slot="survey", bufs=PACK))
             nc.sync.dma_start(survey[s][:], survey_rows[s // PACK, s % PACK])
 
         def load_page(s):
             page.append(tile("page%d" % s, [P, T2], F32))
             nc.sync.dma_start(page[s][:], page_rows[s // PACK, s % PACK])
 
-        def load_factor(i):
-            first, count = factor_first[i], factor[i].shape[1]
+        def load_factor(first_t):
+            count = factor[first_t].shape[1]
             for q in range(QUADS):
-                nc.sync.dma_start(factor[i][32 * q : 32 * q + 32, :, :], wgs_rows[:, first : first + count, :])
+                nc.sync.dma_start(factor[first_t][quadrant(q, 32), :, :], wgs_rows[:, first_t : first_t + count, :])
 
         def factor_of(t):
             return factor[min(t, 2)][:, max(t - 2, 0), :]
@@ -92,25 +101,26 @@ def tile_list_parcel_page_scores_kernel(
         nc.sync.dma_start(w1_raw[0][:], w1_rows[:, :, half(0)])
         load_survey(0)
         load_factor(0)
-        put = lists.tile([P, S // 16], U16, name="put")
+        put = lists.tile([P, S // LIST_ROWS], U16, name="put")
         nc.sync.dma_start(put[:], offs2)
         load_survey(1)
         load_page(0)
         load_factor(1)
-        fetch = lists.tile([P, M // 16], U16, name="fetch")
+        fetch = lists.tile([P, M // LIST_ROWS], U16, name="fetch")
         nc.sync.dma_start(fetch[:], offs3)
         caps = tile("caps", [P, GROUPS, PACK], F32)
         nc.sync.dma_start(caps[:], cap.rearrange("(g p t) -> p g t", p=P, t=PACK))
-        load_survey(2)
         load_factor(2)
+        load_survey(2)
         nc.sync.dma_start(w1_raw[1][:], w1_rows[:, :, half(1)])
         load_page(1)
         load_survey(3)
-        w3_raw = tile("w3_raw", [P, GROUPS, PACK, N], F32, tag="w3raw_capped1")
+        w3_raw = tile("w3_raw", [P, GROUPS, PACK, N], F32, slot="w3_then_capped")
         nc.sync.dma_start(w3_raw[:], w3.rearrange("(g p i) n -> p g i n", p=P, i=PACK))
         load_page(2)
         load_survey(4)
         load_page(3)
+        load_survey(5)
         w4_codes = tile("w4_codes", [P, GROUPS * N], U32)
         nc.sync.dma_start(
             w4_codes[:].bitcast(I32).rearrange("p (g n) -> p g n", g=GROUPS),
@@ -120,17 +130,13 @@ def tile_list_parcel_page_scores_kernel(
         nc.vector.memset(w4_scale[:].bitcast(I32), 0)
         for q in range(QUADS):
             nc.sync.dma_start(
-                w4_scale[32 * q : 32 * q + 4, :].bitcast(I32).rearrange("p (g n) -> p g n", g=GROUPS),
-                w4_scales[:, 4 * q : 4 * q + 4, :].rearrange("g r n -> r g n").bitcast(I32),
+                w4_scale[quadrant(q, 4), :].bitcast(I32).rearrange("p (g n) -> p g n", g=GROUPS),
+                w4_scales[:, scale_rows(q), :].rearrange("g b n -> b g n").bitcast(I32),
             )
-        for s in range(PACK, SLICES):
-            if s + 1 < SLICES:
-                load_survey(s + 1)
-            load_page(s)
-
-        warm = tile("warm", [P, 1], F32)
-        nc.vector.memset(warm[:], 1.0)
-        nc.scalar.activation(warm[:], warm[:], ACT.Abs_reciprocal_sqrt)
+        load_page(4)
+        load_survey(6)
+        load_page(5)
+        load_survey(7)
 
         w2_codes = tile("w2_codes", [P, 2 * H], U8)
         nc.vector.tensor_copy(
@@ -148,13 +154,13 @@ def tile_list_parcel_page_scores_kernel(
             nc.vector.tensor_copy(v_codes[h][:], table[:].indirect(pick[:, list_half(h)]))
             nc.vector.tensor_copy(v_scale[h][:], table_scale[:].indirect(pick[:, list_half(h)]))
 
-        w_scale = tile("w_scale", [P, H + GROUPS * N], U8)
-        w_first = [0, 4 * P, H, H + GROUPS * N]
-        w_bf_slot = ["wide_bf", "work2", "work1"]
-        w_bf, w_codes = {}, {}
+        w_first = [0, BANK, H, H + GROUPS * N]
+        w_scale = tile("w_scale", [P, w_first[3]], U8)
+        w_rounded_slot = ["x_woven", "work2", "work1"]
+        w_rounded, w_codes = {}, {}
 
         def w_part(col):
-            return max(i for i in range(3) if w_first[i] <= col)
+            return max(part for part in range(3) if w_first[part] <= col)
 
         def w_operand(col):
             part = w_part(col)
@@ -163,19 +169,15 @@ def tile_list_parcel_page_scores_kernel(
 
         def open_w(part):
             cols = w_first[part + 1] - w_first[part]
-            w_bf[part] = tile("w_bf%d" % part, [P, PACK * cols], BF16, tag=w_bf_slot[part])
+            w_rounded[part] = tile("w_rounded%d" % part, [P, PACK * cols], BF16, slot=w_rounded_slot[part])
 
-        def round_w1(s0, s1):
-            part = w_part(s0 * P)
-            first = s0 * P - w_first[part]
-            g, t0 = divmod(s0, PACK)
-            dst = w_bf[part][:, first * PACK : (first + (s1 - s0) * P) * PACK]
-            src = w1_raw[g][:].rearrange("p i (q t) -> p q t i", t=PACK)
-            nc.scalar.copy(dst.rearrange("p (t q i) -> p q t i", q=P, i=PACK), src[:, :, t0 : t0 + s1 - s0, :])
+        def round_w1(g, t0, t1):
+            dst = w_rounded[g][:, t0 * P * PACK : t1 * P * PACK].rearrange("p (t q i) -> p q t i", q=P, i=PACK)
+            nc.scalar.copy(dst, w1_raw[g][:].rearrange("p i (q t) -> p q t i", t=PACK)[:, :, t0:t1, :])
 
         def round_w3():
             nc.scalar.copy(
-                w_bf[2][:].rearrange("p (g c j i) -> p g c i j", g=GROUPS, j=PACK, i=PACK),
+                w_rounded[2][:].rearrange("p (g c j i) -> p g c i j", g=GROUPS, j=PACK, i=PACK),
                 w3_raw[:].rearrange("p g i (c j) -> p g c i j", j=PACK),
             )
 
@@ -186,28 +188,24 @@ def tile_list_parcel_page_scores_kernel(
             lo, hi = c0 - w_first[part], c1 - w_first[part]
             nc.vector.quantize_mx(
                 out=w_codes[part][:, lo:hi].bitcast(FP8X4), scales=w_scale[:, c0:c1],
-                in_=w_bf[part][:, lo * PACK : hi * PACK],
+                in_=w_rounded[part][:, lo * PACK : hi * PACK],
             )
 
         open_w(0)
-        round_w1(0, 1)
+        round_w1(0, 0, 1)
         quantize_w(0, P)
-        round_w1(1, PACK)
+        round_w1(0, 1, PACK)
         quantize_w(P, 2 * P)
         quantize_w(2 * P, 4 * P)
 
-        values = {}
-        capped = [tile("capped0", [P, PACK * M], BF16), None]
-        pairs = {}
-        x_codes = {}
-        x_bf = {}
+        values_slot = ["work0", "work1", "work0", "work2", "work0", "work2", "work1", "x_woven"]
+        fetched_slot = ["work0", "w_codes1", "work0", "work2", "w_codes2", "x_codes0", "plane_codes"]
+        values, pairs, woven, plane_codes, x_codes, x_woven = {}, {}, {}, {}, {}, {}
+        capped = {0: tile("capped0", [P, PACK * M], BF16)}
         x_scale = [tile("x_scale%d" % g, [P, M], U8) for g in range(GROUPS)]
-        plane_scale = tile("plane_scale", [P, GROUPS * T2], U8, tag="scales")
-        values_slot = ["work0", "work1", "work0", "work2", "work0", "work2", "work1", "wide_bf"]
-        fetched_slot = ["work0", "w_codes1", "work0", "work2", "w_codes2", "x_codes0", "plane_codes", "w3raw_capped1"]
+        plane_scale = tile("plane_scale", [P, GROUPS * T2], U8, slot="scales")
 
         def products(s, h):
-            cols = slice(s * P, (s + 1) * P)
             first = psum.tile([P, BANK], F32, name="first", tag="bank")
             codes, scale = w_operand(s * P)
             nc.tensor.matmul_mx(
@@ -217,30 +215,29 @@ def tile_list_parcel_page_scores_kernel(
             second = psum.tile([P, BANK], F32, name="second", tag="bank")
             nc.tensor.matmul_mx(
                 out=second[:], lhsT=w2_codes[:, 2 * s * P : 2 * (s + 1) * P].bitcast(FP4X4),
-                lhsT_scale=w2_scale[:, cols],
+                lhsT_scale=w2_scale[:, s * P : (s + 1) * P],
                 rhs=v_codes[h][:].bitcast(FP8X4), rhs_scale=v_scale[h][:], start=True, stop=True,
             )
             return first, second
 
-        def make_values(s):
-            values[s] = tile("values%d" % s, [P, S], F32, tag=values_slot[s])
-            mapped = tile("mapped%d" % s, [P, S], F32, tag="mapped", bufs=2)
-            second_sb = tile("second_sb%d" % s, [P, S], F32, tag="second_sb", bufs=2)
+        def form_values(s):
+            values[s] = tile("values%d" % s, [P, S], F32, slot=values_slot[s])
+            mapped = tile("mapped%d" % s, [P, S], F32, slot="mapped", bufs=AHEAD)
+            second_sb = tile("second_sb%d" % s, [P, S], F32, slot="second_sb", bufs=AHEAD)
             val, wg = values[s], factor_of(s % PACK)
-            c0, c1 = half(0), half(1)
-            first, second = products(s, 0)
-            nc.vector.tensor_tensor(mapped[:, c0], first[:], survey[s][:, c0], ALU.add)
-            if s == 0:
-                nc.vector.tensor_tensor(val[:, c0], second[:], wg[:, c0], ALU.mult)
-                nc.vector.tensor_tensor(val[:, c0], val[:, c0], mapped[:, c0], ALU.mult)
-            else:
-                nc.scalar.copy(second_sb[:, c0], second[:])
-            first, second = products(s, 1)
-            nc.scalar.copy(second_sb[:, c1], second[:])
-            nc.scalar.copy(mapped[:, c1], first[:])
-            c = c1 if s == 0 else slice(0, S)
+            for h in range(2):
+                first, second = products(s, h)
+                c = half(h)
+                if s == 0 and h == 0:
+                    nc.vector.tensor_tensor(mapped[:, c], first[:], survey[s][:, c], ALU.add)
+                    nc.vector.tensor_tensor(val[:, c], second[:], wg[:, c], ALU.mult)
+                    nc.vector.tensor_tensor(val[:, c], val[:, c], mapped[:, c], ALU.mult)
+                else:
+                    nc.scalar.copy(second_sb[:, c], second[:])
+                    nc.scalar.copy(mapped[:, c], first[:])
+            c = half(1) if s == 0 else slice(0, S)
             nc.gpsimd.tensor_tensor(val[:, c], second_sb[:, c], wg[:, c], ALU.mult)
-            nc.gpsimd.tensor_tensor(mapped[:, c1], mapped[:, c1], survey[s][:, c1], ALU.add)
+            nc.gpsimd.tensor_tensor(mapped[:, c], mapped[:, c], survey[s][:, c], ALU.add)
             nc.gpsimd.tensor_tensor(val[:, c], val[:, c], mapped[:, c], ALU.mult)
 
         def scatter(s):
@@ -250,154 +247,157 @@ def tile_list_parcel_page_scores_kernel(
             else:
                 nc.vector.tensor_copy(page[s][:].indirect(put[:]), values[s][:])
 
-        def quantize_x(g, cols, woven_x):
-            nc.vector.quantize_mx(out=x_codes[g][:, cols].bitcast(FP8X4), scales=x_scale[g][:, cols], in_=woven_x[:])
-
-        def weave_x(name, slot, g, count, cols):
-            woven_x = tile(name, [P, PACK * (cols.stop - cols.start)], BF16, tag=slot)
-            src = capped[g][:].rearrange("p (t c i) -> p c t i", t=count, i=PACK)
-            dst = woven_x[:].rearrange("p (c i t) -> p c t i", t=PACK, i=PACK)
-            nc.scalar.copy(dst[:, :, 0:count, :], src[:, cols.start // PACK : cols.stop // PACK, :, :])
-            return woven_x
-
         def fetch_and_cap(s):
             g, t = divmod(s, PACK)
             if s == PACK:
-                capped[1] = tile("capped1", [P, (PACK - 1) * M], BF16, tag="w3raw_capped1")
-            if s == SLICES - 1:
-                x_codes[g] = tile("x_codes1", [P, M], U32)
-                for h in range(2):
-                    fetched = tile("fetched7_%d" % h, [P, BANK], F32, tag=("w3raw_capped1", "work1")[h])
-                    last = x_bf[g][h][:].rearrange("p (m t) -> p m t", t=PACK)
-                    nc.vector.tensor_copy(fetched[:], page[s][:].indirect(fetch[:, list_half(h)]))
-                    nc.vector.tensor_scalar(last[:, :, t], fetched[:], caps[:, g, t : t + 1], None, ALU.min)
-                    quantize_x(g, half(h), x_bf[g][h])
-            else:
-                fetched = tile("fetched%d" % s, [P, M], F32, tag=fetched_slot[s])
-                nc.vector.tensor_copy(fetched[:], page[s][:].indirect(fetch[:]))
-                nc.vector.tensor_scalar(capped[g][:, t * M : (t + 1) * M], fetched[:], caps[:, g, t : t + 1], None, ALU.min)
+                capped[g] = tile("capped1", [P, (PACK - 1) * M], BF16, slot="w3_then_capped")
+            fetched = tile("fetched%d" % s, [P, M], F32, slot=fetched_slot[s])
+            nc.vector.tensor_copy(fetched[:], page[s][:].indirect(fetch[:]))
+            nc.vector.tensor_scalar(capped[g][:, t * M : (t + 1) * M], fetched[:], caps[:, g, t : t + 1], None, ALU.min)
 
-        def round_page(s):
+        def weave_x(name, slot, g, rows, cols):
+            dst = tile(name, [P, PACK * (cols.stop - cols.start)], BF16, slot=slot)
+            src = capped[g][:].rearrange("p (t c i) -> p c t i", t=rows, i=PACK)
+            nc.scalar.copy(
+                dst[:].rearrange("p (c i t) -> p c t i", t=PACK, i=PACK)[:, :, 0:rows, :],
+                src[:, cols.start // PACK : cols.stop // PACK, :, :],
+            )
+            return dst
+
+        def quantize_x(g, cols, src):
+            nc.vector.quantize_mx(out=x_codes[g][:, cols].bitcast(FP8X4), scales=x_scale[g][:, cols], in_=src[:])
+
+        def fetch_cap_quantize_last():
+            g, t = divmod(LAST, PACK)
+            x_codes[g] = tile("x_codes1", [P, M], U32)
+            for h in range(2):
+                fetched = tile("fetched_last%d" % h, [P, BANK], F32, slot=("w3_then_capped", "work1")[h])
+                places = x_woven[g][h][:].rearrange("p (m t) -> p m t", t=PACK)
+                nc.vector.tensor_copy(fetched[:], page[LAST][:].indirect(fetch[:, list_half(h)]))
+                nc.vector.tensor_scalar(places[:, :, t], fetched[:], caps[:, g, t : t + 1], None, ALU.min)
+                quantize_x(g, half(h), x_woven[g][h])
+
+        def round_and_store_page(s):
             g, t = divmod(s, PACK)
             if t == 0:
-                pairs[g] = tile("pairs%d" % g, [P, PACK * T2], BF16, tag="table_pairs")
-            dst = pairs[g][:].rearrange("p (u m e) -> p u m e", u=2, e=2)
-            nc.scalar.copy(dst[:, t // 2, :, t % 2], page[s][:])
+                pairs[g] = tile("pairs%d" % g, [P, PACK * T2], BF16, slot="table_then_pairs")
+            nc.scalar.copy(pairs[g][:].rearrange("p (u m e) -> p u m e", u=2, e=2)[:, t // 2, :, t % 2], page[s][:])
             nc.sync.dma_start(out_rows[g, t], page[s][:])
 
-        woven, plane_codes = {}, {}
-        width = T2 // 2
+        def plane_cols(part):
+            return slice(part * PLANE_PART, (part + 1) * PLANE_PART)
 
-        def weave_page(g, h, copy):
-            woven[g, h] = tile("woven%d_%d" % (g, h), [P, PACK * width], BF16, tag="woven%d" % h)
+        def weave_page(g, part, copy):
+            woven[g, part] = tile("woven%d_%d" % (g, part), [P, PACK * PLANE_PART], BF16, slot="woven%d" % part)
             copy(
-                woven[g, h][:].bitcast(F32).rearrange("p (m u) -> p m u", u=2),
-                pairs[g][:].bitcast(F32).rearrange("p (u m) -> p m u", u=2)[:, h * width : (h + 1) * width, :],
+                woven[g, part][:].bitcast(F32).rearrange("p (m u) -> p m u", u=2),
+                pairs[g][:].bitcast(F32).rearrange("p (u m) -> p m u", u=2)[:, plane_cols(part), :],
             )
 
-        def page_planes(g, h):
-            if h == 0:
-                plane_codes[g] = tile("plane_codes%d" % g, [P, T2], U32, tag=("plane_codes", "page0")[g])
-            codes = plane_codes[g][:, h * width : (h + 1) * width]
+        def quantize_page(g, part):
+            if part == 0:
+                plane_codes[g] = tile("plane_codes%d" % g, [P, T2], U32, slot=("plane_codes", "page0")[g])
+            cols = plane_cols(part)
+            codes = plane_codes[g][:, cols]
             nc.vector.quantize_mx(
-                out=codes.bitcast(FP8X4),
-                scales=plane_scale[:, g * T2 + h * width : g * T2 + (h + 1) * width],
-                in_=woven[g, h][:],
+                out=codes.bitcast(FP8X4), scales=plane_scale[:, g * T2 + cols.start : g * T2 + cols.stop],
+                in_=woven[g, part][:],
             )
-            nc.sync.dma_start(
-                out_2[g, :, h * width : (h + 1) * width, :].rearrange("p m t -> p (m t)").bitcast(I32),
-                codes.bitcast(I32),
-            )
+            nc.sync.dma_start(out_2[g, :, cols, :].rearrange("p m t -> p (m t)").bitcast(I32), codes.bitcast(I32))
 
-        units = [(h, b) for h in range(2) for b in range(N // P)]
-        top, spread = {}, {}
+        row_pieces = N // P
+        pieces = [(h, b) for h in range(2) for b in range(row_pieces)]
+        early_tops = BANKS - len(pieces)
+        top, spread, scores = {}, {}, {}
 
-        def score_pass(sums, codes, scale, unit, g):
-            h = unit[0]
+        def score_pass(sums, codes, scale, piece, g):
+            h = piece[0]
             if g == 0:
-                sums[unit] = psum.tile([P, BANK], F32, name="score", tag="bank")
+                sums[piece] = psum.tile([P, BANK], F32, name="score", tag="bank")
             nc.tensor.matmul_mx(
-                out=sums[unit][:], lhsT=codes, lhsT_scale=scale,
+                out=sums[piece][:], lhsT=codes, lhsT_scale=scale,
                 rhs=x_codes[g][:, half(h)].bitcast(FP8X4), rhs_scale=x_scale[g][:, half(h)],
                 start=(g == 0), stop=(g == GROUPS - 1),
             )
 
-        def top_pass(unit, g):
-            score_pass(top, *w_operand(H + g * N + unit[1] * P), unit, g)
+        def top_pass(piece, g):
+            score_pass(top, *w_operand(H + g * N + piece[1] * P), piece, g)
 
-        def spread_pass(unit, g):
-            cols = slice(g * N + unit[1] * P, g * N + (unit[1] + 1) * P)
-            score_pass(spread, w4_codes[:, cols].bitcast(FP8X4), w4_scale[:, cols], unit, g)
+        def spread_pass(piece, g):
+            cols = slice(g * N + piece[1] * P, g * N + (piece[1] + 1) * P)
+            score_pass(spread, w4_codes[:, cols].bitcast(FP8X4), w4_scale[:, cols], piece, g)
 
-        def finish(unit, square_on_scalar):
-            h, b = unit
+        def finish(piece):
+            h, b = piece
             if b == 0:
-                scores[h] = tile("scores%d" % h, [P, N // P * BANK], F32, tag="page%d" % (1 + h))
-            work = scores[h][:, b * BANK : (b + 1) * BANK]
-            nc.scalar.activation(work, spread[unit][:], ACT.Abs)
-            nc.scalar.activation(work, work, ACT.Abs_reciprocal_sqrt, bias=1.0)
-            if square_on_scalar:
-                nc.scalar.activation(work, work, ACT.Square)
-                nc.vector.tensor_tensor(work, top[unit][:], work, ALU.mult)
-            else:
-                once = tile("once", [P, BANK], F32, tag="mapped", bufs=2)
-                nc.vector.tensor_tensor(once[:], top[unit][:], work, ALU.mult)
-                nc.vector.tensor_tensor(work, once[:], work, ALU.mult)
-            nc.sync.dma_start(out_0[b * P : (b + 1) * P, half(h)], work)
+                scores[h] = tile("scores%d" % h, [P, row_pieces * BANK], F32, slot="page%d" % (1 + h))
+            score = scores[h][:, b * BANK : (b + 1) * BANK]
+            nc.scalar.activation(score, spread[piece][:], ACT.Abs)
+            nc.scalar.activation(score, score, ACT.Abs_reciprocal_sqrt, bias=1.0)
+            nc.scalar.activation(score, score, ACT.Square)
+            nc.vector.tensor_tensor(score, top[piece][:], score, ALU.mult)
+            nc.sync.dma_start(out_0[b * P : (b + 1) * P, half(h)], score)
 
-        scores = {}
-        make_values(0)
-        make_values(1)
-        open_w(1)
-        round_w1(PACK, SLICES)
-        for s in range(SLICES):
-            scatter(s)
-            if s == SLICES - 1:
-                round_page(s)
-            fetch_and_cap(s)
+        def quantize_after_cap(s):
             if s == 1:
                 quantize_w(w_first[1], w_first[2])
-            if s == 3:
-                x_bf[0] = weave_x("x_bf0", "wide_bf", 0, PACK, slice(0, M))
             if s == 4:
                 quantize_w(H, H + BANK)
                 quantize_w(H + BANK, w_first[3])
             if s == 5:
                 x_codes[0] = tile("x_codes0", [P, M], U32)
-                quantize_x(0, slice(0, M), x_bf[0])
+                quantize_x(0, slice(0, M), x_woven[0])
             if s == 6:
-                page_planes(0, 0)
-                page_planes(0, 1)
-                x_bf[1] = [weave_x("x_bf1_%d" % h, ("work1", "work0")[h], 1, PACK - 1, half(h)) for h in range(2)]
-            if s + 2 < SLICES:
-                make_values(s + 2)
-            if s < SLICES - 1:
-                round_page(s)
-            if s == 1:
+                quantize_page(0, 0)
+                quantize_page(0, 1)
+
+        for s in range(AHEAD):
+            form_values(s)
+        open_w(1)
+        round_w1(1, 0, PACK)
+        for s in range(LAST):
+            scatter(s)
+            fetch_and_cap(s)
+            quantize_after_cap(s)
+            if s == PACK - 1:
+                x_woven[0] = weave_x("x_woven0", "x_woven", 0, PACK, slice(0, M))
+            if s == LAST - 1:
+                x_woven[1] = [
+                    weave_x("x_woven1_%d" % h, ("work1", "work0")[h], 1, PACK - 1, half(h)) for h in range(2)
+                ]
+            if s + AHEAD < SLICES:
+                form_values(s + AHEAD)
+            if s in (PACK, PACK + 1):
+                weave_page(0, s - PACK, nc.scalar.copy)
+            round_and_store_page(s)
+            if s in (1, 3):
+                load_page(len(page))
+            if s == 2:
                 open_w(2)
                 round_w3()
-            if s == 3:
-                weave_page(0, 0, nc.scalar.copy)
-                weave_page(0, 1, nc.scalar.copy)
-            if s == 6:
-                for unit in units:
-                    spread_pass(unit, 0)
-                for unit in units[:2]:
-                    top_pass(unit, 0)
+
+        for piece in pieces:
+            spread_pass(piece, 0)
+        for piece in pieces[:early_tops]:
+            top_pass(piece, 0)
+        scatter(LAST)
+        round_and_store_page(LAST)
+        fetch_cap_quantize_last()
 
         for part in range(2):
             weave_page(1, part, nc.vector.tensor_copy)
-            page_planes(1, part)
+            quantize_page(1, part)
         for q in range(QUADS):
             nc.sync.dma_start(
-                out_3[:, 4 * q : 4 * q + 4, :].rearrange("g r m -> r g m").bitcast(I32),
-                plane_scale[32 * q : 32 * q + 4, :].bitcast(I32).rearrange("p (g m) -> p g m", g=GROUPS),
+                out_3[:, scale_rows(q), :].rearrange("g b m -> b g m").bitcast(I32),
+                plane_scale[quadrant(q, 4), :].bitcast(I32).rearrange("p (g m) -> p g m", g=GROUPS),
             )
         for h in range(2):
-            for unit in units[3 * h : 3 * h + 3]:
-                spread_pass(unit, 1)
-            for i in range(3 * h, 3 * h + 3):
-                if i >= 2:
-                    top_pass(units[i], 0)
-                top_pass(units[i], 1)
-                finish(units[i], i < 6)
+            half_pieces = pieces[row_pieces * h : row_pieces * (h + 1)]
+            for piece in half_pieces:
+                spread_pass(piece, 1)
+            for piece in half_pieces:
+                if piece not in top:
+                    top_pass(piece, 0)
+                top_pass(piece, 1)
+                finish(piece)

from contextlib import ExitStack

import concourse.mybir as mybir

K, T, S, H, T2, M, N = 512, 4096, 1024, 1024, 2048, 1024, 384
FLOPS = 2 * 2 * K * H * S + 2 * 2 * H * N * M

F32 = mybir.dt.float32
BF16 = mybir.dt.bfloat16
I32 = mybir.dt.int32
U32 = mybir.dt.uint32
U16 = mybir.dt.uint16
U8 = mybir.dt.uint8
FP8X4 = mybir.dt.float8_e4m3fn_x4
FP4X4 = mybir.dt.float4_e2m1fn_x4
ALU = mybir.AluOpType
ACT = mybir.ActivationFunctionType

P = 128
PACK = 4
GROUPS = H // (P * PACK)
SLICES = GROUPS * PACK
LAST = SLICES - 1
BANK = 512
BANKS = 8
QUADS = 4
LIST_ROWS = 16
PLANE_PART = T2 // 2
AHEAD = 2


def tile_list_parcel_page_scores_kernel(
    tc, tab_words, tab_scales, offs, w1, w2_words, w2_scales, survey_map, wgs, page0, offs2, offs3, cap, w3,
    w4_words, w4_scales, out_0, out_1, out_2, out_3,
):
    nc = tc.nc
    with ExitStack() as ctx:
        lists = ctx.enter_context(tc.tile_pool(name="lists", bufs=1))
        sb = ctx.enter_context(tc.tile_pool(name="sb", bufs=1))
        psum = ctx.enter_context(tc.psum_pool(name="psum", bufs=BANKS))

        def tile(name, shape, dtype, slot=None, bufs=1):
            return sb.tile(shape, dtype, name=name, tag=slot or name, bufs=bufs, align_bytes=64)

        def half(h):
            return slice(h * BANK, (h + 1) * BANK)

        def list_half(h):
            return slice(h * BANK // LIST_ROWS, (h + 1) * BANK // LIST_ROWS)

        def quadrant(q, rows):
            return slice(32 * q, 32 * q + rows)

        def scale_rows(q):
            return slice(4 * q, 4 * q + 4)

        table = tile("table", [P, T], U32, slot="table_then_pairs")
        nc.sync.dma_start(table[:].bitcast(I32), tab_words[0].rearrange("p t i -> p (t i)").bitcast(I32))
        w2_raw = tile("w2_raw", [P, 2 * H], U8)
        nc.scalar.dma_start(w2_raw[:].bitcast(I32), w2_words[0].bitcast(I32))
        w2_scale_raw = tile("w2_scale_raw", [P, H], U8)
        for q in range(QUADS):
            nc.scalar.dma_start(
                w2_scale_raw[quadrant(q, 32), :].bitcast(I32),
                w2_scales[0, scale_rows(q), :].bitcast(I32).partition_broadcast(8),
            )
        pick = lists.tile([P, S // LIST_ROWS], U16, name="pick")
        nc.sync.dma_start(pick[:], offs)
        table_scale = tile("table_scale", [P, T], U8, slot="scales")
        nc.vector.memset(table_scale[:].bitcast(I32), 0)
        for q in range(QUADS):
            nc.gpsimd.dma_start(
                table_scale[quadrant(q, 4), :].bitcast(I32), tab_scales[0, scale_rows(q), :].bitcast(I32)
            )

        w1_rows = w1.rearrange("(p i) r -> p i r", i=PACK)
        w1_raw = [tile("w1_raw%d" % g, [P, PACK, BANK], F32, slot="woven%d" % g) for g in range(GROUPS)]
        survey_rows = survey_map.rearrange("(g p t) j -> g t p j", p=P, t=PACK)
        page_rows = page0.rearrange("(g p t) m -> g t p m", p=P, t=PACK)
        out_rows = out_1.rearrange("(g p t) m -> g t p m", p=P, t=PACK)
        wgs_rows = wgs.rearrange("(q t) j -> q t j", t=PACK)
        factor = [tile("factor0", [P, 1, S], F32), tile("factor1", [P, 1, S], F32), tile("factor23", [P, 2, S], F32)]
        survey, page = [], []

        def load_survey(s):
            survey.append(tile("survey%d" % s, [P, S], F32, slot="survey", bufs=PACK))
            nc.sync.dma_start(survey[s][:], survey_rows[s // PACK, s % PACK])

        def load_page(s):
            page.append(tile("page%d" % s, [P, T2], F32))
            nc.sync.dma_start(page[s][:], page_rows[s // PACK, s % PACK])

        def load_factor(first_t):
            count = factor[first_t].shape[1]
            for q in range(QUADS):
                nc.sync.dma_start(factor[first_t][quadrant(q, 32), :, :], wgs_rows[:, first_t : first_t + count, :])

        def factor_of(t):
            return factor[min(t, 2)][:, max(t - 2, 0), :]

        nc.sync.dma_start(w1_raw[0][:], w1_rows[:, :, half(0)])
        load_survey(0)
        load_factor(0)
        put = lists.tile([P, S // LIST_ROWS], U16, name="put")
        nc.sync.dma_start(put[:], offs2)
        load_survey(1)
        load_page(0)
        load_factor(1)
        fetch = lists.tile([P, M // LIST_ROWS], U16, name="fetch")
        nc.sync.dma_start(fetch[:], offs3)
        caps = tile("caps", [P, GROUPS, PACK], F32)
        nc.sync.dma_start(caps[:], cap.rearrange("(g p t) -> p g t", p=P, t=PACK))
        load_factor(2)
        load_survey(2)
        nc.sync.dma_start(w1_raw[1][:], w1_rows[:, :, half(1)])
        load_page(1)
        load_survey(3)
        w3_raw = tile("w3_raw", [P, GROUPS, PACK, N], F32, slot="w3_then_capped")
        nc.sync.dma_start(w3_raw[:], w3.rearrange("(g p i) n -> p g i n", p=P, i=PACK))
        load_page(2)
        load_survey(4)
        load_page(3)
        load_survey(5)
        w4_codes = tile("w4_codes", [P, GROUPS * N], U32)
        nc.sync.dma_start(
            w4_codes[:].bitcast(I32).rearrange("p (g n) -> p g n", g=GROUPS),
            w4_words.rearrange("g p n i -> p g (n i)").bitcast(I32),
        )
        w4_scale = tile("w4_scale", [P, GROUPS * N], U8)
        nc.vector.memset(w4_scale[:].bitcast(I32), 0)
        for q in range(QUADS):
            nc.sync.dma_start(
                w4_scale[quadrant(q, 4), :].bitcast(I32).rearrange("p (g n) -> p g n", g=GROUPS),
                w4_scales[:, scale_rows(q), :].rearrange("g b n -> b g n").bitcast(I32),
            )
        load_page(4)
        load_survey(6)
        load_page(5)
        load_survey(7)

        w2_codes = tile("w2_codes", [P, 2 * H], U8)
        nc.vector.tensor_copy(
            w2_codes[:].rearrange("p (g t q b) -> p g t q b", g=GROUPS, t=PACK, b=2),
            w2_raw[:].rearrange("p (g q t b) -> p g t q b", g=GROUPS, t=PACK, b=2),
        )
        w2_scale = tile("w2_scale", [P, H], U8)
        nc.vector.tensor_copy(
            w2_scale[:].rearrange("p (g t q) -> p g t q", g=GROUPS, t=PACK),
            w2_scale_raw[:].rearrange("p (g q t) -> p g t q", g=GROUPS, t=PACK),
        )
        v_codes = [tile("v_codes%d" % h, [P, BANK], U32) for h in range(2)]
        v_scale = [tile("v_scale%d" % h, [P, BANK], U8) for h in range(2)]
        for h in range(2):
            nc.vector.tensor_copy(v_codes[h][:], table[:].indirect(pick[:, list_half(h)]))
            nc.vector.tensor_copy(v_scale[h][:], table_scale[:].indirect(pick[:, list_half(h)]))

        w_first = [0, BANK, H, H + GROUPS * N]
        w_scale = tile("w_scale", [P, w_first[3]], U8)
        w_rounded_slot = ["x_woven", "work2", "work1"]
        w_rounded, w_codes = {}, {}

        def w_part(col):
            return max(part for part in range(3) if w_first[part] <= col)

        def w_operand(col):
            part = w_part(col)
            first = col - w_first[part]
            return w_codes[part][:, first : first + P].bitcast(FP8X4), w_scale[:, col : col + P]

        def open_w(part):
            cols = w_first[part + 1] - w_first[part]
            w_rounded[part] = tile("w_rounded%d" % part, [P, PACK * cols], BF16, slot=w_rounded_slot[part])

        def round_w1(g, t0, t1):
            dst = w_rounded[g][:, t0 * P * PACK : t1 * P * PACK].rearrange("p (t q i) -> p q t i", q=P, i=PACK)
            nc.scalar.copy(dst, w1_raw[g][:].rearrange("p i (q t) -> p q t i", t=PACK)[:, :, t0:t1, :])

        def round_w3():
            nc.scalar.copy(
                w_rounded[2][:].rearrange("p (g c j i) -> p g c i j", g=GROUPS, j=PACK, i=PACK),
                w3_raw[:].rearrange("p g i (c j) -> p g c i j", j=PACK),
            )

        def quantize_w(c0, c1):
            part = w_part(c0)
            if part not in w_codes:
                w_codes[part] = tile("w_codes%d" % part, [P, w_first[part + 1] - w_first[part]], U32)
            lo, hi = c0 - w_first[part], c1 - w_first[part]
            nc.vector.quantize_mx(
                out=w_codes[part][:, lo:hi].bitcast(FP8X4), scales=w_scale[:, c0:c1],
                in_=w_rounded[part][:, lo * PACK : hi * PACK],
            )

        open_w(0)
        round_w1(0, 0, 1)
        quantize_w(0, P)
        round_w1(0, 1, PACK)
        quantize_w(P, 2 * P)
        quantize_w(2 * P, 4 * P)

        values_slot = ["work0", "work1", "work0", "work2", "work0", "work2", "work1", "x_woven"]
        fetched_slot = ["work0", "w_codes1", "work0", "work2", "w_codes2", "x_codes0", "plane_codes"]
        values, pairs, woven, plane_codes, x_codes, x_woven = {}, {}, {}, {}, {}, {}
        capped = {0: tile("capped0", [P, PACK * M], BF16)}
        x_scale = [tile("x_scale%d" % g, [P, M], U8) for g in range(GROUPS)]
        plane_scale = tile("plane_scale", [P, GROUPS * T2], U8, slot="scales")

        def products(s, h):
            first = psum.tile([P, BANK], F32, name="first", tag="bank")
            codes, scale = w_operand(s * P)
            nc.tensor.matmul_mx(
                out=first[:], lhsT=codes, lhsT_scale=scale,
                rhs=v_codes[h][:].bitcast(FP8X4), rhs_scale=v_scale[h][:], start=True, stop=True,
            )
            second = psum.tile([P, BANK], F32, name="second", tag="bank")
            nc.tensor.matmul_mx(
                out=second[:], lhsT=w2_codes[:, 2 * s * P : 2 * (s + 1) * P].bitcast(FP4X4),
                lhsT_scale=w2_scale[:, s * P : (s + 1) * P],
                rhs=v_codes[h][:].bitcast(FP8X4), rhs_scale=v_scale[h][:], start=True, stop=True,
            )
            return first, second

        def form_values(s):
            values[s] = tile("values%d" % s, [P, S], F32, slot=values_slot[s])
            mapped = tile("mapped%d" % s, [P, S], F32, slot="mapped", bufs=AHEAD)
            second_sb = tile("second_sb%d" % s, [P, S], F32, slot="second_sb", bufs=AHEAD)
            val, wg = values[s], factor_of(s % PACK)
            for h in range(2):
                first, second = products(s, h)
                c = half(h)
                if s == 0 and h == 0:
                    nc.vector.tensor_tensor(mapped[:, c], first[:], survey[s][:, c], ALU.add)
                    nc.vector.tensor_tensor(val[:, c], second[:], wg[:, c], ALU.mult)
                    nc.vector.tensor_tensor(val[:, c], val[:, c], mapped[:, c], ALU.mult)
                else:
                    nc.scalar.copy(second_sb[:, c], second[:])
                    nc.scalar.copy(mapped[:, c], first[:])
            c = half(1) if s == 0 else slice(0, S)
            nc.gpsimd.tensor_tensor(val[:, c], second_sb[:, c], wg[:, c], ALU.mult)
            nc.gpsimd.tensor_tensor(mapped[:, c], mapped[:, c], survey[s][:, c], ALU.add)
            nc.gpsimd.tensor_tensor(val[:, c], val[:, c], mapped[:, c], ALU.mult)

        def scatter(s):
            if s == 0:
                for h in range(2):
                    nc.vector.tensor_copy(page[s][:].indirect(put[:, list_half(h)]), values[s][:, half(h)])
            else:
                nc.vector.tensor_copy(page[s][:].indirect(put[:]), values[s][:])

        def fetch_and_cap(s):
            g, t = divmod(s, PACK)
            if s == PACK:
                capped[g] = tile("capped1", [P, (PACK - 1) * M], BF16, slot="w3_then_capped")
            fetched = tile("fetched%d" % s, [P, M], F32, slot=fetched_slot[s])
            nc.vector.tensor_copy(fetched[:], page[s][:].indirect(fetch[:]))
            nc.vector.tensor_scalar(capped[g][:, t * M : (t + 1) * M], fetched[:], caps[:, g, t : t + 1], None, ALU.min)

        def weave_x(name, slot, g, rows, cols):
            dst = tile(name, [P, PACK * (cols.stop - cols.start)], BF16, slot=slot)
            src = capped[g][:].rearrange("p (t c i) -> p c t i", t=rows, i=PACK)
            nc.scalar.copy(
                dst[:].rearrange("p (c i t) -> p c t i", t=PACK, i=PACK)[:, :, 0:rows, :],
                src[:, cols.start // PACK : cols.stop // PACK, :, :],
            )
            return dst

        def quantize_x(g, cols, src):
            nc.vector.quantize_mx(out=x_codes[g][:, cols].bitcast(FP8X4), scales=x_scale[g][:, cols], in_=src[:])

        def fetch_cap_quantize_last():
            g, t = divmod(LAST, PACK)
            x_codes[g] = tile("x_codes1", [P, M], U32)
            for h in range(2):
                fetched = tile("fetched_last%d" % h, [P, BANK], F32, slot=("w3_then_capped", "work1")[h])
                places = x_woven[g][h][:].rearrange("p (m t) -> p m t", t=PACK)
                nc.vector.tensor_copy(fetched[:], page[LAST][:].indirect(fetch[:, list_half(h)]))
                nc.vector.tensor_scalar(places[:, :, t], fetched[:], caps[:, g, t : t + 1], None, ALU.min)
                quantize_x(g, half(h), x_woven[g][h])

        def round_and_store_page(s):
            g, t = divmod(s, PACK)
            if t == 0:
                pairs[g] = tile("pairs%d" % g, [P, PACK * T2], BF16, slot="table_then_pairs")
            nc.scalar.copy(pairs[g][:].rearrange("p (u m e) -> p u m e", u=2, e=2)[:, t // 2, :, t % 2], page[s][:])
            nc.sync.dma_start(out_rows[g, t], page[s][:])

        def plane_cols(part):
            return slice(part * PLANE_PART, (part + 1) * PLANE_PART)

        def weave_page(g, part, copy):
            woven[g, part] = tile("woven%d_%d" % (g, part), [P, PACK * PLANE_PART], BF16, slot="woven%d" % part)
            copy(
                woven[g, part][:].bitcast(F32).rearrange("p (m u) -> p m u", u=2),
                pairs[g][:].bitcast(F32).rearrange("p (u m) -> p m u", u=2)[:, plane_cols(part), :],
            )

        def quantize_page(g, part):
            if part == 0:
                plane_codes[g] = tile("plane_codes%d" % g, [P, T2], U32, slot=("plane_codes", "page0")[g])
            cols = plane_cols(part)
            codes = plane_codes[g][:, cols]
            nc.vector.quantize_mx(
                out=codes.bitcast(FP8X4), scales=plane_scale[:, g * T2 + cols.start : g * T2 + cols.stop],
                in_=woven[g, part][:],
            )
            nc.sync.dma_start(out_2[g, :, cols, :].rearrange("p m t -> p (m t)").bitcast(I32), codes.bitcast(I32))

        row_pieces = N // P
        pieces = [(h, b) for h in range(2) for b in range(row_pieces)]
        early_tops = BANKS - len(pieces)
        top, spread, scores = {}, {}, {}

        def score_pass(sums, codes, scale, piece, g):
            h = piece[0]
            if g == 0:
                sums[piece] = psum.tile([P, BANK], F32, name="score", tag="bank")
            nc.tensor.matmul_mx(
                out=sums[piece][:], lhsT=codes, lhsT_scale=scale,
                rhs=x_codes[g][:, half(h)].bitcast(FP8X4), rhs_scale=x_scale[g][:, half(h)],
                start=(g == 0), stop=(g == GROUPS - 1),
            )

        def top_pass(piece, g):
            score_pass(top, *w_operand(H + g * N + piece[1] * P), piece, g)

        def spread_pass(piece, g):
            cols = slice(g * N + piece[1] * P, g * N + (piece[1] + 1) * P)
            score_pass(spread, w4_codes[:, cols].bitcast(FP8X4), w4_scale[:, cols], piece, g)

        def finish(piece):
            h, b = piece
            if b == 0:
                scores[h] = tile("scores%d" % h, [P, row_pieces * BANK], F32, slot="page%d" % (1 + h))
            score = scores[h][:, b * BANK : (b + 1) * BANK]
            nc.scalar.activation(score, spread[piece][:], ACT.Abs)
            nc.scalar.activation(score, score, ACT.Abs_reciprocal_sqrt, bias=1.0)
            nc.scalar.activation(score, score, ACT.Square)
            nc.vector.tensor_tensor(score, top[piece][:], score, ALU.mult)
            nc.sync.dma_start(out_0[b * P : (b + 1) * P, half(h)], score)

        def quantize_after_cap(s):
            if s == 1:
                quantize_w(w_first[1], w_first[2])
            if s == 4:
                quantize_w(H, H + BANK)
                quantize_w(H + BANK, w_first[3])
            if s == 5:
                x_codes[0] = tile("x_codes0", [P, M], U32)
                quantize_x(0, slice(0, M), x_woven[0])
            if s == 6:
                quantize_page(0, 0)
                quantize_page(0, 1)

        for s in range(AHEAD):
            form_values(s)
        open_w(1)
        round_w1(1, 0, PACK)
        for s in range(LAST):
            scatter(s)
            fetch_and_cap(s)
            quantize_after_cap(s)
            if s == PACK - 1:
                x_woven[0] = weave_x("x_woven0", "x_woven", 0, PACK, slice(0, M))
            if s == LAST - 1:
                x_woven[1] = [
                    weave_x("x_woven1_%d" % h, ("work1", "work0")[h], 1, PACK - 1, half(h)) for h in range(2)
                ]
            if s + AHEAD < SLICES:
                form_values(s + AHEAD)
            if s in (PACK, PACK + 1):
                weave_page(0, s - PACK, nc.scalar.copy)
            round_and_store_page(s)
            if s in (1, 3):
                load_page(len(page))
            if s == 2:
                open_w(2)
                round_w3()

        for piece in pieces:
            spread_pass(piece, 0)
        for piece in pieces[:early_tops]:
            top_pass(piece, 0)
        scatter(LAST)
        round_and_store_page(LAST)
        fetch_cap_quantize_last()

        for part in range(2):
            weave_page(1, part, nc.vector.tensor_copy)
            quantize_page(1, part)
        for q in range(QUADS):
            nc.sync.dma_start(
                out_3[:, scale_rows(q), :].rearrange("g b m -> b g m").bitcast(I32),
                plane_scale[quadrant(q, 4), :].bitcast(I32).rearrange("p (g m) -> p g m", g=GROUPS),
            )
        for h in range(2):
            half_pieces = pieces[row_pieces * h : row_pieces * (h + 1)]
            for piece in half_pieces:
                spread_pass(piece, 1)
            for piece in half_pieces:
                if piece not in top:
                    top_pass(piece, 0)
                top_pass(piece, 1)
                finish(piece)
